import numpy as np
import ml_dtypes


def mxq(x, axis, fmt="e4m3"):
    dtype, down = {"e4m3": (ml_dtypes.float8_e4m3fn, 7), "e5m2": (ml_dtypes.float8_e5m2, 14)}[fmt]
    v = np.moveaxis(np.asarray(x, np.float32).astype(ml_dtypes.bfloat16).astype(np.float64), axis, -1)
    blocks = v.reshape(v.shape[:-1] + (-1, 32))
    amax = np.abs(blocks).max(-1, keepdims=True)
    byte = np.maximum(np.where(amax > 0, np.frexp(amax)[1] - 1 + 127, 0) - down, 1)
    scale = np.exp2(byte - 127.0)
    codes = (blocks / scale).astype(np.float32).astype(dtype).astype(np.float64)
    return np.moveaxis((codes * scale).reshape(v.shape), -1, axis)


WIDE = False


def mx_kscale(k):
    if not WIDE:
        return np.ones(k)
    levels = np.array([10, -10, 5, -5, 0])
    if k % 512:
        return np.exp2(np.random.permutation(np.resize(levels, k // 32))).repeat(32)
    a = np.empty((k // 512, 16))
    for p in range(k // 512):
        a[p, :8] = np.random.permutation(np.resize(levels, 8))
        for g in range(8):
            far = levels[np.abs(levels - a[p, g]) >= 10]
            a[p, g + 8] = far[np.random.randint(len(far))]
    return np.exp2(a.ravel()).repeat(32)


def f64(x):
    return np.asarray(x).astype(np.float64)


def striped(idx):
    return np.tile(idx.reshape(-1, 16).T, (8, 1)).astype(np.uint16)


def unstriped(offs):
    return offs[:16].T.reshape(-1).astype(np.int64)


E2M1 = np.array([0.0, 0.5, 1.0, 1.5, 2.0, 3.0, 4.0, 6.0, -0.0, -0.5, -1.0, -1.5, -2.0, -3.0, -4.0, -6.0])


def pack_weight(w, fmt):
    k, n = w.shape
    w = f64(np.asarray(w, np.float32).astype(ml_dtypes.bfloat16)).reshape(k // 32, 32, n)
    amax = np.abs(w).max(1)
    if fmt == "e4m3":
        byte = np.frexp(amax)[1] - 1 + 127 - 7
    else:
        mant, ex = np.frexp(amax / 6.0)
        byte = np.where(mant > 0.5, ex, ex - 1) + 127
    byte = np.clip(np.where(amax > 0, byte, 1), 1, 254)
    scaled = (w * np.exp2(127.0 - byte)[:, None, :]).reshape(k, n).astype(np.float32)
    by_word = np.ascontiguousarray(scaled.reshape(k // 512, 128, 4, n).transpose(0, 1, 3, 2))
    if fmt == "e4m3":
        words = by_word.astype(ml_dtypes.float8_e4m3fn).view(np.uint8)
    else:
        c = by_word.astype(ml_dtypes.float4_e2m1fn).view(np.uint8) & 0xF
        words = (c[..., 0::2] | (c[..., 1::2] << 4)).reshape(k // 512, 128, 2 * n)
    return np.ascontiguousarray(words), np.ascontiguousarray(byte.astype(np.uint8).reshape(k // 512, 16, n))


def unpack_weight(words, scales, fmt):
    g, _, n = scales.shape
    words = np.ascontiguousarray(words).reshape(g, 128, n, -1)
    if fmt == "e4m3":
        vals = words.view(ml_dtypes.float8_e4m3fn).astype(np.float64)
    else:
        nib = np.empty((g, 128, n, 4), np.uint8)
        nib[..., 0::2] = words & 0xF
        nib[..., 1::2] = words >> 4
        vals = E2M1[nib]
    vals = vals * np.repeat(np.exp2(scales.astype(np.float64) - 127.0), 8, axis=1)[..., None]
    return vals.transpose(0, 1, 3, 2).reshape(g * 512, n)


def gelu(v):
    return 0.5 * v * (1.0 + np.tanh(np.sqrt(2.0 / np.pi) * (v + 0.044715 * v**3)))


def striped8(idx):
    return np.concatenate([v.reshape(-1, 16).T for v in idx]).astype(np.uint16)


def unstriped8(offs):
    return np.stack([offs[16 * g:16 * g + 16].T.reshape(-1) for g in range(8)]).astype(np.int64)


def runs(v, idx8):
    k = np.arange(v.shape[0])
    return v[k[:, None], idx8[k % 512 // 64]]


K, K2, H, N, T, S, T2 = 1024, 512, 1024, 512, 2048, 512, 1024

def setup_inputs():
    n = np.random.standard_normal
    s, s2, u = mx_kscale(K)[:, None], mx_kscale(K2)[:, None], mx_kscale(H)[:, None]
    tab_words, tab_scales = pack_weight(n((K, T)) * s, "e4m3")
    tab2_words, tab2_scales = pack_weight(n((K2, T)) * s2, "e4m3")
    w2_words, w2_scales = pack_weight(1.2 * n((K2, H)) / np.sqrt(K2) / s2, "e2m1")
    return {
        "tab_words": tab_words, "tab_scales": tab_scales,
        "tab2_words": tab2_words, "tab2_scales": tab2_scales,
        "offs": striped8(np.stack([np.random.permutation(T)[:S] for _ in range(8)])),
        "offs2": striped(np.random.permutation(T)[:S]),
        "offs3": striped(np.random.permutation(T2)[:S]),
        "w1": (1.2 * n((K, H)) / np.sqrt(K) / s).astype(np.float32),
        "w2_words": w2_words, "w2_scales": w2_scales,
        "b1": (0.5 * n(H)).astype(np.float32),
        "hgain": (np.exp(0.3 * n(H)) * u[:, 0]).astype(np.float32),
        "w4": (1.3 * n((H, N)) / np.sqrt(H) / u).astype(np.float32),
        "desk": np.exp(0.4 * n(N)).astype(np.float32),
        "w3": (0.8 * n((K, N)) / np.sqrt(K) / s).astype(np.float32),
        "page1": n((N, T2)).astype(np.float32),
        "wgo": np.exp(0.3 * n((128, S))).astype(np.float32),
    }

def reference(tab_words, tab_scales, tab2_words, tab2_scales, offs, offs2, offs3, w1, w2_words, w2_scales,
              b1, hgain, w4, desk, w3, page1, wgo):
    v = runs(unpack_weight(tab_words, tab_scales, "e4m3"), unstriped8(offs))
    v2 = unpack_weight(tab2_words, tab2_scales, "e4m3")[:, unstriped(offs2)]
    w2 = unpack_weight(w2_words, w2_scales, "e2m1")
    a = mxq(f64(w1), 0, "e4m3").T @ v + w2.T @ v2
    h = np.tanh(a + f64(b1)[:, None]) * f64(hgain)[:, None]
    p = mxq(f64(w4), 0, "e4m3").T @ mxq(h, 0, "e4m3")
    q = mxq(f64(w3), 0, "e4m3").T @ v
    y = f64(desk)[:, None] * p + q
    out = f64(page1).copy()
    out[:, unstriped(offs3)] = np.tile(f64(wgo), (N // 128, 1)) * y
    return out

@@ -1,0 +1,270 @@
+from contextlib import ExitStack
+
+import concourse.mybir as mybir
+
+K, K2, H, N, T, S, T2 = 1024, 512, 1024, 512, 2048, 512, 1024
+FLOPS = 2 * S * (K * H + K2 * H + H * N + K * N)
+
+F32 = mybir.dt.float32
+BF16 = mybir.dt.bfloat16
+I32 = mybir.dt.int32
+U32 = mybir.dt.uint32
+U16 = mybir.dt.uint16
+U8 = mybir.dt.uint8
+E4M3X4 = mybir.dt.float8_e4m3fn_x4
+E2M1X4 = mybir.dt.float4_e2m1fn_x4
+MULT = mybir.AluOpType.mult
+ADD = mybir.AluOpType.add
+TANH = mybir.ActivationFunctionType.Tanh
+
+P = 128
+PACK = 4
+K_PASS = P * PACK
+HALF = S // 2
+W_COLS = 256
+W1_VECTOR_SHARE = 80
+
+
+def tile_list_photo_caption_consistency_kernel(
+    tc, tab_words, tab_scales, tab2_words, tab2_scales, offs, offs2, offs3, w1, w2_words, w2_scales,
+    b1, hgain, w4, desk, w3, page1, wgo, out,
+):
+    nc = tc.nc
+    with ExitStack() as ctx:
+        keep = ctx.enter_context(tc.tile_pool(name="keep", bufs=1))
+        stage = ctx.enter_context(tc.tile_pool(name="stage", bufs=2))
+        psum = ctx.enter_context(tc.psum_pool(name="psum", bufs=8))
+
+        def held(name, shape, dtype):
+            return keep.tile(shape, dtype, name=name, align_bytes=64)
+
+        v_scale_win = [held("v_scale_win%d" % a, [P, T], U8) for a in range(2)]
+        v2_scale_win = held("v2_scale_win", [P, T], U8)
+        w2_scale_raw = held("w2_scale_raw", [P, H], U8)
+        scale_loads = [(v_scale_win[0], tab_scales[0]), (v_scale_win[1], tab_scales[1]),
+                       (v2_scale_win, tab2_scales[0]), (w2_scale_raw, w2_scales[0])]
+        for tile, rows in scale_loads:
+            nc.vector.memset(tile[:].bitcast(I32), 0)
+
+        list1 = held("list1", [P, S // 16], U16)
+        list2 = held("list2", [P, S // 16], U16)
+        list3 = held("list3", [P, S // 16], U16)
+        v_win = [held("v_win%d" % a, [P, T], U32) for a in range(2)]
+        v2_win = held("v2_win", [P, T], U32)
+        w2_raw = held("w2_raw", [P, H], U16)
+        w1_raw = {(a, b): held("w1_raw%d%d" % (a, b), [P, PACK, K_PASS], F32) for a in range(2) for b in range(2)}
+        w3_raw = {(a, c): held("w3_raw%d%d" % (a, c), [P, PACK, W_COLS], F32) for a in range(2) for c in range(2)}
+        w4_raw = {(a, c): held("w4_raw%d%d" % (a, c), [P, PACK, W_COLS], F32) for a in range(2) for c in range(2)}
+        bias = held("bias", [P, 2, PACK], F32)
+        gain = held("gain", [P, 2, PACK], F32)
+        desk_cols = held("desk_cols", [P, N // P], F32)
+        wgo_rows = held("wgo_rows", [P, S], F32)
+        pages = [held("page%d" % u, [P, T2], F32) for u in range(N // P)]
+
+        def load_words(tile, words, col0=0, width=T):
+            nc.sync.dma_start(out=tile[:, col0:col0 + width].bitcast(I32),
+                              in_=words[:, col0:col0 + width, :].rearrange("p t i -> p (t i)").bitcast(I32))
+
+        def load_weight(tile, w, a, col0, width):
+            rows = w[a * K_PASS:(a + 1) * K_PASS, col0:col0 + width]
+            nc.sync.dma_start(out=tile[:], in_=rows.rearrange("(p j) c -> p j c", j=PACK))
+
+        def load_page(u):
+            nc.sync.dma_start(out=pages[u][:], in_=page1[u * P:(u + 1) * P, :])
+
+        nc.sync.dma_start(list1[:], offs)
+        load_weight(w1_raw[0, 0], w1, 0, 0, K_PASS)
+        for tile, rows in scale_loads:
+            nc.sync.dma_start(out=tile[0:P:8, :].bitcast(I32), in_=rows.bitcast(I32))
+        nc.sync.dma_start(list2[:], offs2)
+        nc.sync.dma_start(out=w2_raw[:].bitcast(I32), in_=w2_words[0].bitcast(I32))
+        load_words(v_win[0], tab_words[0], 0, T // 2)
+        load_words(v_win[0], tab_words[0], T // 2, T // 2)
+        nc.sync.dma_start(out=bias[:], in_=b1.rearrange("(b p t) -> p b t", b=2, t=PACK))
+        nc.sync.dma_start(out=gain[:], in_=hgain.rearrange("(b p t) -> p b t", b=2, t=PACK))
+        with nc.allow_non_contiguous_dma(reason="one value of desk for each partition and row tile"):
+            nc.sync.dma_start(out=desk_cols[:], in_=desk.rearrange("(u p) -> p u", p=P))
+        nc.sync.dma_start(list3[:], offs3)
+        load_weight(w1_raw[1, 0], w1, 1, 0, K_PASS)
+        load_words(v_win[1], tab_words[1])
+
+        v_scale_got = held("v_scale_got", [P, 2, S], U8)
+        v2_scale_got = held("v2_scale_got", [P, S], U8)
+        planes = held("planes", [P, 3 * S + H], U8)
+        for a in range(2):
+            nc.vector.tensor_copy(v_scale_got[:, a, :], v_scale_win[a][:].indirect(list1[:]))
+        nc.vector.tensor_copy(v2_scale_got[:], v2_scale_win[:].indirect(list2[:]))
+        nc.vector.tensor_copy(planes[:, 0:2 * S].bitcast(I32),
+                              v_scale_got[:].rearrange("p a s -> p (a s)").bitcast(I32))
+        nc.vector.tensor_copy(planes[:, 2 * S:3 * S].bitcast(I32), v2_scale_got[:].bitcast(I32))
+        nc.vector.tensor_copy(planes[:, 3 * S:].rearrange("p (b t m) -> p b t m", b=2, t=PACK),
+                              w2_scale_raw[:].rearrange("p (b m t) -> p b t m", b=2, t=PACK))
+        for r in range(1, 4):
+            nc.sync.dma_start(out=planes[r:P:32, :].bitcast(I32), in_=planes[8 * r:P:32, :].bitcast(I32))
+        load_words(v2_win, tab2_words[0])
+        load_weight(w1_raw[0, 1], w1, 0, K_PASS, K_PASS)
+        load_weight(w1_raw[1, 1], w1, 1, K_PASS, K_PASS)
+        for a in range(2):
+            load_weight(w3_raw[a, 0], w3, a, 0, W_COLS)
+        for a in range(2):
+            load_weight(w4_raw[a, 0], w4, a, 0, W_COLS)
+        nc.sync.dma_start(out=wgo_rows[:], in_=wgo)
+        load_page(0)
+        load_page(1)
+        for a in range(2):
+            load_weight(w3_raw[a, 1], w3, a, W_COLS, W_COLS)
+        for a in range(2):
+            load_weight(w4_raw[a, 1], w4, a, W_COLS, W_COLS)
+        load_page(2)
+        load_page(3)
+        v_plane = [planes[:, a * S:(a + 1) * S] for a in range(2)]
+        v2_plane = planes[:, 2 * S:3 * S]
+
+        w1_codes = {}
+        w1_plane = {}
+
+        def round_w1(a, b, vector_share):
+            grouped = stage.tile([P, PACK, P, PACK], BF16, name="w1_grouped", align_bytes=64)
+            src = w1_raw[a, b][:].rearrange("p j (m t) -> p m j t", t=PACK)
+            dst = grouped[:].rearrange("p t m j -> p m j t")
+            if vector_share > 0:
+                nc.vector.tensor_copy(dst[:, 0:vector_share], src[:, 0:vector_share])
+            if vector_share < P:
+                nc.scalar.copy(dst[:, vector_share:P], src[:, vector_share:P])
+            return grouped
+
+        def quantise_w1(a, b, grouped):
+            w1_codes[a, b] = held("w1_codes%d%d" % (a, b), [P, K_PASS], U32)
+            w1_plane[a, b] = held("w1_plane%d%d" % (a, b), [P, K_PASS], U8)
+            nc.vector.quantize_mx(out=w1_codes[a, b][:].bitcast(E4M3X4), scales=w1_plane[a, b][:],
+                                  in_=grouped[:].rearrange("p t m j -> p (t m j)"))
+
+        v_codes = [held("v_codes%d" % a, [P, S], U32) for a in range(2)]
+        v2_codes = held("v2_codes", [P, S], U32)
+        w2_dealt = held("w2_dealt", [P, H], U16)
+        a_sum = {}
+
+        def pass_w1(a, b, start, stop):
+            for t in range(PACK):
+                cols = slice(t * P, (t + 1) * P)
+                nc.tensor.matmul_mx(out=a_sum[b, t][:], lhsT=w1_codes[a, b][:, cols].bitcast(E4M3X4),
+                                    lhsT_scale=w1_plane[a, b][:, cols], rhs=v_codes[a][:].bitcast(E4M3X4),
+                                    rhs_scale=v_plane[a], start=start, stop=stop)
+
+        def pass_w2(b, start, stop):
+            for t in range(PACK):
+                col0 = b * K_PASS + t * P
+                nc.tensor.matmul_mx(out=a_sum[b, t][:], lhsT=w2_dealt[:, col0:col0 + P].bitcast(E2M1X4),
+                                    lhsT_scale=planes[:, 3 * S + col0:3 * S + col0 + P],
+                                    rhs=v2_codes[:].bitcast(E4M3X4), rhs_scale=v2_plane, start=start, stop=stop)
+
+        h_codes = [held("h_codes%d" % b, [P, S], U32) for b in range(2)]
+        h_plane = [held("h_plane%d" % b, [P, S], U8) for b in range(2)]
+
+        def tanh_half(b, s):
+            th = stage.tile([P, PACK, HALF], F32, name="th")
+            for t in range(PACK):
+                nc.scalar.activation(th[:, t, :], a_sum[b, t][:, s * HALF:(s + 1) * HALF], TANH,
+                                     bias=bias[:, b, t:t + 1])
+            return th
+
+        def gain_half(b, th):
+            grouped = stage.tile([P, HALF, PACK], BF16, name="h_grouped", align_bytes=64)
+            nc.vector.tensor_tensor(
+                grouped[:].rearrange("p (c i) t -> p c t i", i=4),
+                th[:].rearrange("p t (c i) -> p c t i", i=4),
+                gain[:, b, :].unsqueeze(1).unsqueeze(3).broadcast_to([P, HALF // 4, PACK, 4]),
+                MULT)
+            return grouped
+
+        def quantise_h(b, s, grouped):
+            cols = slice(s * HALF, (s + 1) * HALF)
+            nc.vector.quantize_mx(out=h_codes[b][:, cols].bitcast(E4M3X4), scales=h_plane[b][:, cols],
+                                  in_=grouped[:].rearrange("p c t -> p (c t)"))
+
+        def round_out_weight(raw, u, pool, name):
+            grouped = pool.tile([P, 2, P, PACK], BF16, name=name, align_bytes=64)
+            c, col0 = divmod(u * P, W_COLS)
+            for a in range(2):
+                src = raw[a, c][:, :, col0:col0 + P].rearrange("p j (c i) -> p c j i", i=4)
+                dst = grouped[:, a].rearrange("p (c i) j -> p c j i", i=4)
+                nc.scalar.copy(dst, src)
+            return grouped
+
+        def quantise_out_weight(grouped, name):
+            codes = stage.tile([P, 2 * P], U32, name=name + "_codes", align_bytes=64)
+            plane = stage.tile([P, 2 * P], U8, name=name + "_plane", align_bytes=64)
+            nc.vector.quantize_mx(out=codes[:].bitcast(E4M3X4), scales=plane[:],
+                                  in_=grouped[:].rearrange("p a m j -> p (a m j)"))
+            return codes, plane
+
+        def product(weight, moving_codes, moving_plane, col0, width):
+            codes, plane = weight
+            bank = psum.tile([P, width], F32, name="bank")
+            for a in range(2):
+                cols = slice(a * P, (a + 1) * P)
+                nc.tensor.matmul_mx(out=bank[:], lhsT=codes[:, cols].bitcast(E4M3X4), lhsT_scale=plane[:, cols],
+                                    rhs=moving_codes[a][:, col0:col0 + width].bitcast(E4M3X4),
+                                    rhs_scale=moving_plane[a][:, col0:col0 + width],
+                                    start=(a == 0), stop=(a == 1))
+            return bank
+
+        for b in range(2):
+            for t in range(PACK):
+                a_sum[b, t] = psum.tile([P, S], F32, name="bank")
+
+        g00 = round_w1(0, 0, 0)
+        nc.scalar.copy(w2_dealt[:].rearrange("p (b t m) -> p b t m", b=2, t=PACK),
+                       w2_raw[:].rearrange("p (b m t) -> p b t m", b=2, t=PACK))
+        nc.vector.tensor_copy(v_codes[0][:], v_win[0][:].indirect(list1[:]))
+        quantise_w1(0, 0, g00)
+        pass_w1(0, 0, True, False)
+        g10 = round_w1(1, 0, 0)
+        nc.vector.tensor_copy(v_codes[1][:], v_win[1][:].indirect(list1[:]))
+        quantise_w1(1, 0, g10)
+        pass_w1(1, 0, False, False)
+        nc.vector.tensor_copy(v2_codes[:], v2_win[:].indirect(list2[:]))
+        pass_w2(0, False, True)
+        pass_w2(1, True, False)
+        th0 = [tanh_half(0, s) for s in range(2)]
+        g01 = round_w1(0, 1, P // 2)
+        quantise_w1(0, 1, g01)
+        pass_w1(0, 1, False, False)
+        g11 = round_w1(1, 1, W1_VECTOR_SHARE)
+        quantise_w1(1, 1, g11)
+        pass_w1(1, 1, False, True)
+        for s in range(2):
+            quantise_h(0, s, gain_half(0, th0[s]))
+        th1 = [tanh_half(1, s) for s in range(2)]
+
+        def image_product(u):
+            w3_q = quantise_out_weight(round_out_weight(w3_raw, u, stage, "w3_grouped"), "w3")
+            bank = product(w3_q, v_codes, v_plane, 0, S)
+            q_rows = stage.tile([P, S], F32, name="q_rows")
+            nc.scalar.copy(q_rows[:], bank[:])
+            return q_rows
+
+        def quantise_w4(u):
+            return quantise_out_weight(round_out_weight(w4_raw, u, keep, "w4_grouped_or_y"), "w4")
+
+        def put_half(u, s, p_bank, q_rows, y_half):
+            cols = slice(s * HALF, (s + 1) * HALF)
+            nc.vector.scalar_tensor_tensor(y_half[:], p_bank[:], desk_cols[:, u:u + 1], q_rows[:, cols], MULT, ADD)
+            entries = list3[:, s * HALF // 16:(s + 1) * HALF // 16]
+            nc.vector.tensor_tensor(pages[u][:].indirect(entries), y_half[:], wgo_rows[:, cols], MULT)
+
+        quantise_h(1, 0, gain_half(1, th1[0]))
+        q_rows = image_product(0)
+        w4_q = quantise_w4(0)
+        p_banks = [product(w4_q, h_codes, h_plane, 0, HALF)]
+        quantise_h(1, 1, gain_half(1, th1[1]))
+        p_banks.append(product(w4_q, h_codes, h_plane, HALF, HALF))
+        for u in range(N // P):
+            put_half(u, 0, p_banks[0], q_rows, stage.tile([P, HALF], F32, name="y_first"))
+            if u + 1 < N // P:
+                next_q_rows = image_product(u + 1)
+                w4_q = quantise_w4(u + 1)
+                next_p_banks = [product(w4_q, h_codes, h_plane, s * HALF, HALF) for s in range(2)]
+            put_half(u, 1, p_banks[1], q_rows, keep.tile([P, HALF], F32, name="w4_grouped_or_y", align_bytes=64))
+            nc.sync.dma_start(out=out[u * P:(u + 1) * P, :], in_=pages[u][:])
+            q_rows, p_banks = next_q_rows, next_p_banks

@@ -1,6 +1,7 @@
 from contextlib import ExitStack
 
 import concourse.mybir as mybir
+from concourse.masks import make_identity
 
 K, K2, H, N, T, S, T2 = 1024, 512, 1024, 512, 2048, 512, 1024
 FLOPS = 2 * S * (K * H + K2 * H + H * N + K * N)
@@ -22,7 +23,12 @@ PACK = 4
 K_PASS = P * PACK
 HALF = S // 2
 W_COLS = 256
-W1_VECTOR_SHARE = 80
+SHARE_00 = 0
+SHARE_01 = 64
+SHARE_10 = 64
+SHARE_11 = 96
+FIRST_W3_ON_VECTOR = 0
+FIRST_W4_ON_VECTOR = 1
 
 
 def tile_list_photo_caption_consistency_kernel(
@@ -52,18 +58,21 @@ def tile_list_photo_caption_consistency_kernel(
         v_win = [held("v_win%d" % a, [P, T], U32) for a in range(2)]
         v2_win = held("v2_win", [P, T], U32)
         w2_raw = held("w2_raw", [P, H], U16)
-        w1_raw = {(a, b): held("w1_raw%d%d" % (a, b), [P, PACK, K_PASS], F32) for a in range(2) for b in range(2)}
+        w1_first = held("w1_first", [P, PACK, H], F32)
+        w1_second = [held("w1_second%d" % b, [P, PACK, K_PASS], F32) for b in range(2)]
+        w1_raw = {(0, 0): w1_first[:, :, 0:K_PASS], (0, 1): w1_first[:, :, K_PASS:H],
+                  (1, 0): w1_second[0][:], (1, 1): w1_second[1][:]}
         w3_raw = {(a, c): held("w3_raw%d%d" % (a, c), [P, PACK, W_COLS], F32) for a in range(2) for c in range(2)}
         w4_raw = {(a, c): held("w4_raw%d%d" % (a, c), [P, PACK, W_COLS], F32) for a in range(2) for c in range(2)}
-        bias = held("bias", [P, 2, PACK], F32)
-        gain = held("gain", [P, 2, PACK], F32)
-        desk_cols = held("desk_cols", [P, N // P], F32)
+        vector_rows = held("vector_rows", [P, K_PASS], F32)
+        identity = held("identity", [P, P], F32)
+        nc.gpsimd.memset(vector_rows[:], 0.0)
+        make_identity(nc, identity[:])
         wgo_rows = held("wgo_rows", [P, S], F32)
         pages = [held("page%d" % u, [P, T2], F32) for u in range(N // P)]
 
-        def load_words(tile, words, col0=0, width=T):
-            nc.sync.dma_start(out=tile[:, col0:col0 + width].bitcast(I32),
-                              in_=words[:, col0:col0 + width, :].rearrange("p t i -> p (t i)").bitcast(I32))
+        def load_words(tile, words):
+            nc.sync.dma_start(out=tile[:].bitcast(I32), in_=words.rearrange("p t i -> p (t i)").bitcast(I32))
 
         def load_weight(tile, w, a, col0, width):
             rows = w[a * K_PASS:(a + 1) * K_PASS, col0:col0 + width]
@@ -73,20 +82,16 @@ def tile_list_photo_caption_consistency_kernel(
             nc.sync.dma_start(out=pages[u][:], in_=page1[u * P:(u + 1) * P, :])
 
         nc.sync.dma_start(list1[:], offs)
-        load_weight(w1_raw[0, 0], w1, 0, 0, K_PASS)
+        load_words(v_win[0], tab_words[0])
         for tile, rows in scale_loads:
             nc.sync.dma_start(out=tile[0:P:8, :].bitcast(I32), in_=rows.bitcast(I32))
         nc.sync.dma_start(list2[:], offs2)
+        load_weight(w1_first, w1, 0, 0, H)
         nc.sync.dma_start(out=w2_raw[:].bitcast(I32), in_=w2_words[0].bitcast(I32))
-        load_words(v_win[0], tab_words[0], 0, T // 2)
-        load_words(v_win[0], tab_words[0], T // 2, T // 2)
-        nc.sync.dma_start(out=bias[:], in_=b1.rearrange("(b p t) -> p b t", b=2, t=PACK))
-        nc.sync.dma_start(out=gain[:], in_=hgain.rearrange("(b p t) -> p b t", b=2, t=PACK))
-        with nc.allow_non_contiguous_dma(reason="one value of desk for each partition and row tile"):
-            nc.sync.dma_start(out=desk_cols[:], in_=desk.rearrange("(u p) -> p u", p=P))
-        nc.sync.dma_start(list3[:], offs3)
-        load_weight(w1_raw[1, 0], w1, 1, 0, K_PASS)
-        load_words(v_win[1], tab_words[1])
+        nc.sync.dma_start(out=vector_rows[0:2, :], in_=b1.rearrange("(b r) -> b r", b=2))
+        nc.sync.dma_start(out=vector_rows[2:4, :], in_=hgain.rearrange("(b r) -> b r", b=2))
+        nc.sync.dma_start(out=vector_rows[4:8, 0:P], in_=desk.rearrange("(u p) -> u p", p=P))
+        load_weight(w1_second[0], w1, 1, 0, K_PASS)
 
         v_scale_got = held("v_scale_got", [P, 2, S], U8)
         v2_scale_got = held("v2_scale_got", [P, S], U8)
@@ -101,13 +106,14 @@ def tile_list_photo_caption_consistency_kernel(
                               w2_scale_raw[:].rearrange("p (b m t) -> p b t m", b=2, t=PACK))
         for r in range(1, 4):
             nc.sync.dma_start(out=planes[r:P:32, :].bitcast(I32), in_=planes[8 * r:P:32, :].bitcast(I32))
+        load_words(v_win[1], tab_words[1])
         load_words(v2_win, tab2_words[0])
-        load_weight(w1_raw[0, 1], w1, 0, K_PASS, K_PASS)
-        load_weight(w1_raw[1, 1], w1, 1, K_PASS, K_PASS)
+        load_weight(w1_second[1], w1, 1, K_PASS, K_PASS)
         for a in range(2):
             load_weight(w3_raw[a, 0], w3, a, 0, W_COLS)
         for a in range(2):
             load_weight(w4_raw[a, 0], w4, a, 0, W_COLS)
+        nc.sync.dma_start(list3[:], offs3)
         nc.sync.dma_start(out=wgo_rows[:], in_=wgo)
         load_page(0)
         load_page(1)
@@ -120,12 +126,22 @@ def tile_list_photo_caption_consistency_kernel(
         v_plane = [planes[:, a * S:(a + 1) * S] for a in range(2)]
         v2_plane = planes[:, 2 * S:3 * S]
 
+        turned = psum.tile([P, PACK, P], F32, name="bank")
+        for t in range(PACK):
+            nc.tensor.transpose(turned[:, t, :], vector_rows[:, t:K_PASS:PACK], identity[:])
+        turned_desk = psum.tile([P, P], F32, name="bank")
+        nc.tensor.transpose(turned_desk[:], vector_rows[:, 0:P], identity[:])
+        bias_gain = held("bias_gain", [P, PACK, 4], F32)
+        desk_cols = held("desk_cols", [P, N // P], F32)
+        nc.scalar.copy(bias_gain[:], turned[:, :, 0:4])
+        nc.scalar.copy(desk_cols[:], turned_desk[:, 4:8])
+
         w1_codes = {}
         w1_plane = {}
 
         def round_w1(a, b, vector_share):
             grouped = stage.tile([P, PACK, P, PACK], BF16, name="w1_grouped", align_bytes=64)
-            src = w1_raw[a, b][:].rearrange("p j (m t) -> p m j t", t=PACK)
+            src = w1_raw[a, b].rearrange("p j (m t) -> p m j t", t=PACK)
             dst = grouped[:].rearrange("p t m j -> p m j t")
             if vector_share > 0:
                 nc.vector.tensor_copy(dst[:, 0:vector_share], src[:, 0:vector_share])
@@ -144,28 +160,36 @@ def tile_list_photo_caption_consistency_kernel(
         w2_dealt = held("w2_dealt", [P, H], U16)
         a_sum = {}
 
-        def pass_w1(a, b, start, stop):
-            for t in range(PACK):
-                cols = slice(t * P, (t + 1) * P)
-                nc.tensor.matmul_mx(out=a_sum[b, t][:], lhsT=w1_codes[a, b][:, cols].bitcast(E4M3X4),
-                                    lhsT_scale=w1_plane[a, b][:, cols], rhs=v_codes[a][:].bitcast(E4M3X4),
-                                    rhs_scale=v_plane[a], start=start, stop=stop)
+        def pass_w1(a, b, first, last):
+            for s in range(2):
+                entries = slice(s * HALF, (s + 1) * HALF)
+                for t in range(PACK):
+                    cols = slice(t * P, (t + 1) * P)
+                    nc.tensor.matmul_mx(out=a_sum[b, s, t // 2][:, t % 2, :],
+                                        lhsT=w1_codes[a, b][:, cols].bitcast(E4M3X4),
+                                        lhsT_scale=w1_plane[a, b][:, cols],
+                                        rhs=v_codes[a][:, entries].bitcast(E4M3X4), rhs_scale=v_plane[a][:, entries],
+                                        start=first and t % 2 == 0, stop=last and t % 2 == 1)
 
-        def pass_w2(b, start, stop):
-            for t in range(PACK):
-                col0 = b * K_PASS + t * P
-                nc.tensor.matmul_mx(out=a_sum[b, t][:], lhsT=w2_dealt[:, col0:col0 + P].bitcast(E2M1X4),
-                                    lhsT_scale=planes[:, 3 * S + col0:3 * S + col0 + P],
-                                    rhs=v2_codes[:].bitcast(E4M3X4), rhs_scale=v2_plane, start=start, stop=stop)
+        def pass_w2(b, first, last):
+            for s in range(2):
+                entries = slice(s * HALF, (s + 1) * HALF)
+                for t in range(PACK):
+                    col0 = b * K_PASS + t * P
+                    nc.tensor.matmul_mx(out=a_sum[b, s, t // 2][:, t % 2, :],
+                                        lhsT=w2_dealt[:, col0:col0 + P].bitcast(E2M1X4),
+                                        lhsT_scale=planes[:, 3 * S + col0:3 * S + col0 + P],
+                                        rhs=v2_codes[:, entries].bitcast(E4M3X4), rhs_scale=v2_plane[:, entries],
+                                        start=first and t % 2 == 0, stop=last and t % 2 == 1)
 
         h_codes = [held("h_codes%d" % b, [P, S], U32) for b in range(2)]
         h_plane = [held("h_plane%d" % b, [P, S], U8) for b in range(2)]
 
         def tanh_half(b, s):
-            th = stage.tile([P, PACK, HALF], F32, name="th")
+            th = stage.tile([P, PACK, HALF], F32, name="th", bufs=4)
             for t in range(PACK):
-                nc.scalar.activation(th[:, t, :], a_sum[b, t][:, s * HALF:(s + 1) * HALF], TANH,
-                                     bias=bias[:, b, t:t + 1])
+                nc.scalar.activation(th[:, t, :], a_sum[b, s, t // 2][:, t % 2, :], TANH,
+                                     bias=bias_gain[:, t, b:b + 1])
             return th
 
         def gain_half(b, th):
@@ -173,7 +197,7 @@ def tile_list_photo_caption_consistency_kernel(
             nc.vector.tensor_tensor(
                 grouped[:].rearrange("p (c i) t -> p c t i", i=4),
                 th[:].rearrange("p t (c i) -> p c t i", i=4),
-                gain[:, b, :].unsqueeze(1).unsqueeze(3).broadcast_to([P, HALF // 4, PACK, 4]),
+                bias_gain[:, :, 2 + b].unsqueeze(1).unsqueeze(3).broadcast_to([P, HALF // 4, PACK, 4]),
                 MULT)
             return grouped
 
@@ -182,13 +206,16 @@ def tile_list_photo_caption_consistency_kernel(
             nc.vector.quantize_mx(out=h_codes[b][:, cols].bitcast(E4M3X4), scales=h_plane[b][:, cols],
                                   in_=grouped[:].rearrange("p c t -> p (c t)"))
 
-        def round_out_weight(raw, u, pool, name):
+        def round_out_weight(raw, u, pool, name, on_vector):
             grouped = pool.tile([P, 2, P, PACK], BF16, name=name, align_bytes=64)
             c, col0 = divmod(u * P, W_COLS)
             for a in range(2):
                 src = raw[a, c][:, :, col0:col0 + P].rearrange("p j (c i) -> p c j i", i=4)
                 dst = grouped[:, a].rearrange("p (c i) j -> p c j i", i=4)
-                nc.scalar.copy(dst, src)
+                if a >= 2 - on_vector:
+                    nc.vector.tensor_copy(dst, src)
+                else:
+                    nc.scalar.copy(dst, src)
             return grouped
 
         def quantise_out_weight(grouped, name):
@@ -210,42 +237,40 @@ def tile_list_photo_caption_consistency_kernel(
             return bank
 
         for b in range(2):
-            for t in range(PACK):
-                a_sum[b, t] = psum.tile([P, S], F32, name="bank")
+            for s in range(2):
+                for pair in range(2):
+                    a_sum[b, s, pair] = psum.tile([P, 2, HALF], F32, name="bank")
 
-        g00 = round_w1(0, 0, 0)
+        nc.vector.tensor_copy(v_codes[0][:], v_win[0][:].indirect(list1[:]))
+        quantise_w1(0, 0, round_w1(0, 0, SHARE_00))
+        pass_w1(0, 0, True, False)
         nc.scalar.copy(w2_dealt[:].rearrange("p (b t m) -> p b t m", b=2, t=PACK),
                        w2_raw[:].rearrange("p (b m t) -> p b t m", b=2, t=PACK))
-        nc.vector.tensor_copy(v_codes[0][:], v_win[0][:].indirect(list1[:]))
-        quantise_w1(0, 0, g00)
-        pass_w1(0, 0, True, False)
-        g10 = round_w1(1, 0, 0)
+        quantise_w1(0, 1, round_w1(0, 1, SHARE_01))
+        pass_w1(0, 1, True, False)
+        quantise_w1(1, 0, round_w1(1, 0, SHARE_10))
         nc.vector.tensor_copy(v_codes[1][:], v_win[1][:].indirect(list1[:]))
-        quantise_w1(1, 0, g10)
         pass_w1(1, 0, False, False)
-        nc.vector.tensor_copy(v2_codes[:], v2_win[:].indirect(list2[:]))
-        pass_w2(0, False, True)
-        pass_w2(1, True, False)
-        th0 = [tanh_half(0, s) for s in range(2)]
-        g01 = round_w1(0, 1, P // 2)
-        quantise_w1(0, 1, g01)
-        pass_w1(0, 1, False, False)
-        g11 = round_w1(1, 1, W1_VECTOR_SHARE)
-        quantise_w1(1, 1, g11)
-        pass_w1(1, 1, False, True)
         for s in range(2):
-            quantise_h(0, s, gain_half(0, th0[s]))
-        th1 = [tanh_half(1, s) for s in range(2)]
+            nc.vector.tensor_copy(v2_codes[:, s * HALF:(s + 1) * HALF],
+                                  v2_win[:].indirect(list2[:, s * HALF // 16:(s + 1) * HALF // 16]))
+        pass_w2(0, False, True)
+        pass_w2(1, False, False)
+        quantise_w1(1, 1, round_w1(1, 1, SHARE_11))
+        pass_w1(1, 1, False, True)
+
+        def make_h(b, s):
+            quantise_h(b, s, gain_half(b, tanh_half(b, s)))
 
         def image_product(u):
-            w3_q = quantise_out_weight(round_out_weight(w3_raw, u, stage, "w3_grouped"), "w3")
+            w3_q = quantise_out_weight(round_out_weight(w3_raw, u, stage, "w3_grouped", FIRST_W3_ON_VECTOR if u == 0 else 0), "w3")
             bank = product(w3_q, v_codes, v_plane, 0, S)
             q_rows = stage.tile([P, S], F32, name="q_rows")
             nc.scalar.copy(q_rows[:], bank[:])
             return q_rows
 
         def quantise_w4(u):
-            return quantise_out_weight(round_out_weight(w4_raw, u, keep, "w4_grouped_or_y"), "w4")
+            return quantise_out_weight(round_out_weight(w4_raw, u, keep, "w4_grouped_or_y", FIRST_W4_ON_VECTOR if u == 0 else 0), "w4")
 
         def put_half(u, s, p_bank, q_rows, y_half):
             cols = slice(s * HALF, (s + 1) * HALF)
@@ -253,11 +278,13 @@ def tile_list_photo_caption_consistency_kernel(
             entries = list3[:, s * HALF // 16:(s + 1) * HALF // 16]
             nc.vector.tensor_tensor(pages[u][:].indirect(entries), y_half[:], wgo_rows[:, cols], MULT)
 
-        quantise_h(1, 0, gain_half(1, th1[0]))
+        make_h(0, 0)
+        make_h(0, 1)
+        make_h(1, 0)
         q_rows = image_product(0)
         w4_q = quantise_w4(0)
         p_banks = [product(w4_q, h_codes, h_plane, 0, HALF)]
-        quantise_h(1, 1, gain_half(1, th1[1]))
+        make_h(1, 1)
         p_banks.append(product(w4_q, h_codes, h_plane, HALF, HALF))
         for u in range(N // P):
             put_half(u, 0, p_banks[0], q_rows, stage.tile([P, HALF], F32, name="y_first"))

@@ -24,10 +24,12 @@ K_PASS = P * PACK
 HALF = S // 2
 W_COLS = 256
 SHARE_00 = 0
-SHARE_01 = 64
-SHARE_10 = 64
+SHARE_01 = 128
+ORDER = 0
+H_ORDER = 0
+SHARE_10 = 0
 SHARE_11 = 96
-FIRST_W3_ON_VECTOR = 0
+FIRST_W3_ON_VECTOR = 1
 FIRST_W4_ON_VECTOR = 1
 
 
@@ -58,10 +60,7 @@ def tile_list_photo_caption_consistency_kernel(
         v_win = [held("v_win%d" % a, [P, T], U32) for a in range(2)]
         v2_win = held("v2_win", [P, T], U32)
         w2_raw = held("w2_raw", [P, H], U16)
-        w1_first = held("w1_first", [P, PACK, H], F32)
-        w1_second = [held("w1_second%d" % b, [P, PACK, K_PASS], F32) for b in range(2)]
-        w1_raw = {(0, 0): w1_first[:, :, 0:K_PASS], (0, 1): w1_first[:, :, K_PASS:H],
-                  (1, 0): w1_second[0][:], (1, 1): w1_second[1][:]}
+        w1_raw = {(a, b): held("w1_raw%d%d" % (a, b), [P, PACK, K_PASS], F32)[:] for a in range(2) for b in range(2)}
         w3_raw = {(a, c): held("w3_raw%d%d" % (a, c), [P, PACK, W_COLS], F32) for a in range(2) for c in range(2)}
         w4_raw = {(a, c): held("w4_raw%d%d" % (a, c), [P, PACK, W_COLS], F32) for a in range(2) for c in range(2)}
         vector_rows = held("vector_rows", [P, K_PASS], F32)
@@ -82,16 +81,16 @@ def tile_list_photo_caption_consistency_kernel(
             nc.sync.dma_start(out=pages[u][:], in_=page1[u * P:(u + 1) * P, :])
 
         nc.sync.dma_start(list1[:], offs)
-        load_words(v_win[0], tab_words[0])
+        load_weight(w1_raw[0, 0], w1, 0, 0, K_PASS)
         for tile, rows in scale_loads:
             nc.sync.dma_start(out=tile[0:P:8, :].bitcast(I32), in_=rows.bitcast(I32))
         nc.sync.dma_start(list2[:], offs2)
-        load_weight(w1_first, w1, 0, 0, H)
         nc.sync.dma_start(out=w2_raw[:].bitcast(I32), in_=w2_words[0].bitcast(I32))
+        load_words(v_win[0], tab_words[0])
         nc.sync.dma_start(out=vector_rows[0:2, :], in_=b1.rearrange("(b r) -> b r", b=2))
         nc.sync.dma_start(out=vector_rows[2:4, :], in_=hgain.rearrange("(b r) -> b r", b=2))
         nc.sync.dma_start(out=vector_rows[4:8, 0:P], in_=desk.rearrange("(u p) -> u p", p=P))
-        load_weight(w1_second[0], w1, 1, 0, K_PASS)
+        load_weight(w1_raw[1, 0], w1, 1, 0, K_PASS)
 
         v_scale_got = held("v_scale_got", [P, 2, S], U8)
         v2_scale_got = held("v2_scale_got", [P, S], U8)
@@ -104,25 +103,38 @@ def tile_list_photo_caption_consistency_kernel(
         nc.vector.tensor_copy(planes[:, 2 * S:3 * S].bitcast(I32), v2_scale_got[:].bitcast(I32))
         nc.vector.tensor_copy(planes[:, 3 * S:].rearrange("p (b t m) -> p b t m", b=2, t=PACK),
                               w2_scale_raw[:].rearrange("p (b m t) -> p b t m", b=2, t=PACK))
+        load_words(v_win[1], tab_words[1])
         for r in range(1, 4):
             nc.sync.dma_start(out=planes[r:P:32, :].bitcast(I32), in_=planes[8 * r:P:32, :].bitcast(I32))
-        load_words(v_win[1], tab_words[1])
-        load_words(v2_win, tab2_words[0])
-        load_weight(w1_second[1], w1, 1, K_PASS, K_PASS)
-        for a in range(2):
-            load_weight(w3_raw[a, 0], w3, a, 0, W_COLS)
-        for a in range(2):
-            load_weight(w4_raw[a, 0], w4, a, 0, W_COLS)
-        nc.sync.dma_start(list3[:], offs3)
-        nc.sync.dma_start(out=wgo_rows[:], in_=wgo)
-        load_page(0)
-        load_page(1)
-        for a in range(2):
-            load_weight(w3_raw[a, 1], w3, a, W_COLS, W_COLS)
-        for a in range(2):
-            load_weight(w4_raw[a, 1], w4, a, W_COLS, W_COLS)
-        load_page(2)
-        load_page(3)
+        def ld(x):
+            if x == "A":
+                for a in range(2):
+                    load_weight(w3_raw[a, 0], w3, a, 0, W_COLS)
+            if x == "B":
+                for a in range(2):
+                    load_weight(w4_raw[a, 0], w4, a, 0, W_COLS)
+            if x == "C":
+                for a in range(2):
+                    load_weight(w3_raw[a, 1], w3, a, W_COLS, W_COLS)
+            if x == "D":
+                for a in range(2):
+                    load_weight(w4_raw[a, 1], w4, a, W_COLS, W_COLS)
+            if x == "w":
+                nc.sync.dma_start(list3[:], offs3)
+                nc.sync.dma_start(out=wgo_rows[:], in_=wgo)
+            if x == "t":
+                load_words(v2_win, tab2_words[0])
+            if x == "s":
+                load_weight(w1_raw[0, 1], w1, 0, K_PASS, K_PASS)
+                load_weight(w1_raw[1, 1], w1, 1, K_PASS, K_PASS)
+            if x == "a":
+                load_weight(w3_raw[0, 0], w3, 0, 0, W_COLS)
+            if x == "e":
+                load_weight(w3_raw[1, 0], w3, 1, 0, W_COLS)
+            if x in "0123":
+                load_page(int(x))
+        for x in ["tsABw0CD123", "tsABw01CD23", "tsABw0C1D23", "stABw0CD123", "tsBAw0CD123"][ORDER]:
+            ld(x)
         v_plane = [planes[:, a * S:(a + 1) * S] for a in range(2)]
         v2_plane = planes[:, 2 * S:3 * S]
 
@@ -241,21 +253,21 @@ def tile_list_photo_caption_consistency_kernel(
                 for pair in range(2):
                     a_sum[b, s, pair] = psum.tile([P, 2, HALF], F32, name="bank")
 
-        nc.vector.tensor_copy(v_codes[0][:], v_win[0][:].indirect(list1[:]))
-        quantise_w1(0, 0, round_w1(0, 0, SHARE_00))
-        pass_w1(0, 0, True, False)
         nc.scalar.copy(w2_dealt[:].rearrange("p (b t m) -> p b t m", b=2, t=PACK),
                        w2_raw[:].rearrange("p (b m t) -> p b t m", b=2, t=PACK))
-        quantise_w1(0, 1, round_w1(0, 1, SHARE_01))
-        pass_w1(0, 1, True, False)
-        quantise_w1(1, 0, round_w1(1, 0, SHARE_10))
+        quantise_w1(0, 0, round_w1(0, 0, SHARE_00))
+        nc.vector.tensor_copy(v_codes[0][:], v_win[0][:].indirect(list1[:]))
+        pass_w1(0, 0, True, False)
         nc.vector.tensor_copy(v_codes[1][:], v_win[1][:].indirect(list1[:]))
+        quantise_w1(1, 0, round_w1(1, 0, SHARE_10))
         pass_w1(1, 0, False, False)
         for s in range(2):
             nc.vector.tensor_copy(v2_codes[:, s * HALF:(s + 1) * HALF],
                                   v2_win[:].indirect(list2[:, s * HALF // 16:(s + 1) * HALF // 16]))
         pass_w2(0, False, True)
-        pass_w2(1, False, False)
+        pass_w2(1, True, False)
+        quantise_w1(0, 1, round_w1(0, 1, SHARE_01))
+        pass_w1(0, 1, False, False)
         quantise_w1(1, 1, round_w1(1, 1, SHARE_11))
         pass_w1(1, 1, False, True)
 
@@ -264,34 +276,32 @@ def tile_list_photo_caption_consistency_kernel(
 
         def image_product(u):
             w3_q = quantise_out_weight(round_out_weight(w3_raw, u, stage, "w3_grouped", FIRST_W3_ON_VECTOR if u == 0 else 0), "w3")
-            bank = product(w3_q, v_codes, v_plane, 0, S)
-            q_rows = stage.tile([P, S], F32, name="q_rows")
-            nc.scalar.copy(q_rows[:], bank[:])
-            return q_rows
+            return product(w3_q, v_codes, v_plane, 0, S)
 
         def quantise_w4(u):
-            return quantise_out_weight(round_out_weight(w4_raw, u, keep, "w4_grouped_or_y", FIRST_W4_ON_VECTOR if u == 0 else 0), "w4")
+            return quantise_out_weight(round_out_weight(w4_raw, u, keep, "swap%d" % (u % 2), FIRST_W4_ON_VECTOR if u == 0 else 0), "w4")
 
-        def put_half(u, s, p_bank, q_rows, y_half):
-            cols = slice(s * HALF, (s + 1) * HALF)
-            nc.vector.scalar_tensor_tensor(y_half[:], p_bank[:], desk_cols[:, u:u + 1], q_rows[:, cols], MULT, ADD)
-            entries = list3[:, s * HALF // 16:(s + 1) * HALF // 16]
-            nc.vector.tensor_tensor(pages[u][:].indirect(entries), y_half[:], wgo_rows[:, cols], MULT)
+        def put(u, col0, width, p_bank, q_rows, y):
+            cols = slice(col0, col0 + width)
+            scaled = stage.tile([P, width], F32, name="scaled")
+            nc.scalar.activation(scaled[:], p_bank[:], mybir.ActivationFunctionType.Copy, scale=desk_cols[:, u:u + 1])
+            nc.vector.tensor_tensor(y[:], q_rows[:, cols], scaled[:], ADD)
+            nc.vector.tensor_tensor(pages[u][:].indirect(list3[:, col0 // 16:(col0 + width) // 16]), y[:], wgo_rows[:, cols], MULT)
 
         make_h(0, 0)
         make_h(0, 1)
         make_h(1, 0)
         q_rows = image_product(0)
         w4_q = quantise_w4(0)
-        p_banks = [product(w4_q, h_codes, h_plane, 0, HALF)]
+        p_first = product(w4_q, h_codes, h_plane, 0, HALF)
         make_h(1, 1)
-        p_banks.append(product(w4_q, h_codes, h_plane, HALF, HALF))
+        p_bank = product(w4_q, h_codes, h_plane, HALF, HALF)
+        put(0, 0, HALF, p_first, q_rows, held("y_first", [P, HALF], F32))
         for u in range(N // P):
-            put_half(u, 0, p_banks[0], q_rows, stage.tile([P, HALF], F32, name="y_first"))
+            col0 = HALF if u == 0 else 0
             if u + 1 < N // P:
                 next_q_rows = image_product(u + 1)
-                w4_q = quantise_w4(u + 1)
-                next_p_banks = [product(w4_q, h_codes, h_plane, s * HALF, HALF) for s in range(2)]
-            put_half(u, 1, p_banks[1], q_rows, keep.tile([P, HALF], F32, name="w4_grouped_or_y", align_bytes=64))
+                next_p_bank = product(quantise_w4(u + 1), h_codes, h_plane, 0, S)
+            put(u, col0, S - col0, p_bank, q_rows, held("swap%d" % ((u + 1) % 2), [P, S - col0], F32))
             nc.sync.dma_start(out=out[u * P:(u + 1) * P, :], in_=pages[u][:])
-            q_rows, p_banks = next_q_rows, next_p_banks
+            q_rows, p_bank = next_q_rows, next_p_bank

from contextlib import ExitStack

import concourse.mybir as mybir
from concourse.masks import make_identity

K, K2, H, N, T, S, T2 = 1024, 512, 1024, 512, 2048, 512, 1024
FLOPS = 2 * S * (K * H + K2 * H + H * N + K * N)

F32 = mybir.dt.float32
BF16 = mybir.dt.bfloat16
I32 = mybir.dt.int32
U32 = mybir.dt.uint32
U16 = mybir.dt.uint16
U8 = mybir.dt.uint8
E4M3X4 = mybir.dt.float8_e4m3fn_x4
E2M1X4 = mybir.dt.float4_e2m1fn_x4
MULT = mybir.AluOpType.mult
ADD = mybir.AluOpType.add
TANH = mybir.ActivationFunctionType.Tanh

P = 128
PACK = 4
K_PASS = P * PACK
HALF = S // 2
W_COLS = 256
SHARE_00 = 0
SHARE_01 = 128
ORDER = 0
H_ORDER = 0
SHARE_10 = 0
SHARE_11 = 96
FIRST_W3_ON_VECTOR = 1
FIRST_W4_ON_VECTOR = 1


def tile_list_photo_caption_consistency_kernel(
    tc, tab_words, tab_scales, tab2_words, tab2_scales, offs, offs2, offs3, w1, w2_words, w2_scales,
    b1, hgain, w4, desk, w3, page1, wgo, out,
):
    nc = tc.nc
    with ExitStack() as ctx:
        keep = ctx.enter_context(tc.tile_pool(name="keep", bufs=1))
        stage = ctx.enter_context(tc.tile_pool(name="stage", bufs=2))
        psum = ctx.enter_context(tc.psum_pool(name="psum", bufs=8))

        def held(name, shape, dtype):
            return keep.tile(shape, dtype, name=name, align_bytes=64)

        v_scale_win = [held("v_scale_win%d" % a, [P, T], U8) for a in range(2)]
        v2_scale_win = held("v2_scale_win", [P, T], U8)
        w2_scale_raw = held("w2_scale_raw", [P, H], U8)
        scale_loads = [(v_scale_win[0], tab_scales[0]), (v_scale_win[1], tab_scales[1]),
                       (v2_scale_win, tab2_scales[0]), (w2_scale_raw, w2_scales[0])]
        for tile, rows in scale_loads:
            nc.vector.memset(tile[:].bitcast(I32), 0)

        list1 = held("list1", [P, S // 16], U16)
        list2 = held("list2", [P, S // 16], U16)
        list3 = held("list3", [P, S // 16], U16)
        v_win = [held("v_win%d" % a, [P, T], U32) for a in range(2)]
        v2_win = held("v2_win", [P, T], U32)
        w2_raw = held("w2_raw", [P, H], U16)
        w1_raw = {(a, b): held("w1_raw%d%d" % (a, b), [P, PACK, K_PASS], F32)[:] for a in range(2) for b in range(2)}
        w3_raw = {(a, c): held("w3_raw%d%d" % (a, c), [P, PACK, W_COLS], F32) for a in range(2) for c in range(2)}
        w4_raw = {(a, c): held("w4_raw%d%d" % (a, c), [P, PACK, W_COLS], F32) for a in range(2) for c in range(2)}
        vector_rows = held("vector_rows", [P, K_PASS], F32)
        identity = held("identity", [P, P], F32)
        nc.gpsimd.memset(vector_rows[:], 0.0)
        make_identity(nc, identity[:])
        wgo_rows = held("wgo_rows", [P, S], F32)
        pages = [held("page%d" % u, [P, T2], F32) for u in range(N // P)]

        def load_words(tile, words):
            nc.sync.dma_start(out=tile[:].bitcast(I32), in_=words.rearrange("p t i -> p (t i)").bitcast(I32))

        def load_weight(tile, w, a, col0, width):
            rows = w[a * K_PASS:(a + 1) * K_PASS, col0:col0 + width]
            nc.sync.dma_start(out=tile[:], in_=rows.rearrange("(p j) c -> p j c", j=PACK))

        def load_page(u):
            nc.sync.dma_start(out=pages[u][:], in_=page1[u * P:(u + 1) * P, :])

        nc.sync.dma_start(list1[:], offs)
        load_weight(w1_raw[0, 0], w1, 0, 0, K_PASS)
        for tile, rows in scale_loads:
            nc.sync.dma_start(out=tile[0:P:8, :].bitcast(I32), in_=rows.bitcast(I32))
        nc.sync.dma_start(list2[:], offs2)
        nc.sync.dma_start(out=w2_raw[:].bitcast(I32), in_=w2_words[0].bitcast(I32))
        load_words(v_win[0], tab_words[0])
        nc.sync.dma_start(out=vector_rows[0:2, :], in_=b1.rearrange("(b r) -> b r", b=2))
        nc.sync.dma_start(out=vector_rows[2:4, :], in_=hgain.rearrange("(b r) -> b r", b=2))
        nc.sync.dma_start(out=vector_rows[4:8, 0:P], in_=desk.rearrange("(u p) -> u p", p=P))
        load_weight(w1_raw[1, 0], w1, 1, 0, K_PASS)

        v_scale_got = held("v_scale_got", [P, 2, S], U8)
        v2_scale_got = held("v2_scale_got", [P, S], U8)
        planes = held("planes", [P, 3 * S + H], U8)
        for a in range(2):
            nc.vector.tensor_copy(v_scale_got[:, a, :], v_scale_win[a][:].indirect(list1[:]))
        nc.vector.tensor_copy(v2_scale_got[:], v2_scale_win[:].indirect(list2[:]))
        nc.vector.tensor_copy(planes[:, 0:2 * S].bitcast(I32),
                              v_scale_got[:].rearrange("p a s -> p (a s)").bitcast(I32))
        nc.vector.tensor_copy(planes[:, 2 * S:3 * S].bitcast(I32), v2_scale_got[:].bitcast(I32))
        nc.vector.tensor_copy(planes[:, 3 * S:].rearrange("p (b t m) -> p b t m", b=2, t=PACK),
                              w2_scale_raw[:].rearrange("p (b m t) -> p b t m", b=2, t=PACK))
        load_words(v_win[1], tab_words[1])
        for r in range(1, 4):
            nc.sync.dma_start(out=planes[r:P:32, :].bitcast(I32), in_=planes[8 * r:P:32, :].bitcast(I32))
        def ld(x):
            if x == "A":
                for a in range(2):
                    load_weight(w3_raw[a, 0], w3, a, 0, W_COLS)
            if x == "B":
                for a in range(2):
                    load_weight(w4_raw[a, 0], w4, a, 0, W_COLS)
            if x == "C":
                for a in range(2):
                    load_weight(w3_raw[a, 1], w3, a, W_COLS, W_COLS)
            if x == "D":
                for a in range(2):
                    load_weight(w4_raw[a, 1], w4, a, W_COLS, W_COLS)
            if x == "w":
                nc.sync.dma_start(list3[:], offs3)
                nc.sync.dma_start(out=wgo_rows[:], in_=wgo)
            if x == "t":
                load_words(v2_win, tab2_words[0])
            if x == "s":
                load_weight(w1_raw[0, 1], w1, 0, K_PASS, K_PASS)
                load_weight(w1_raw[1, 1], w1, 1, K_PASS, K_PASS)
            if x == "a":
                load_weight(w3_raw[0, 0], w3, 0, 0, W_COLS)
            if x == "e":
                load_weight(w3_raw[1, 0], w3, 1, 0, W_COLS)
            if x in "0123":
                load_page(int(x))
        for x in ["tsABw0CD123", "tsABw01CD23", "tsABw0C1D23", "stABw0CD123", "tsBAw0CD123"][ORDER]:
            ld(x)
        v_plane = [planes[:, a * S:(a + 1) * S] for a in range(2)]
        v2_plane = planes[:, 2 * S:3 * S]

        turned = psum.tile([P, PACK, P], F32, name="bank")
        for t in range(PACK):
            nc.tensor.transpose(turned[:, t, :], vector_rows[:, t:K_PASS:PACK], identity[:])
        turned_desk = psum.tile([P, P], F32, name="bank")
        nc.tensor.transpose(turned_desk[:], vector_rows[:, 0:P], identity[:])
        bias_gain = held("bias_gain", [P, PACK, 4], F32)
        desk_cols = held("desk_cols", [P, N // P], F32)
        nc.scalar.copy(bias_gain[:], turned[:, :, 0:4])
        nc.scalar.copy(desk_cols[:], turned_desk[:, 4:8])

        w1_codes = {}
        w1_plane = {}

        def round_w1(a, b, vector_share):
            grouped = stage.tile([P, PACK, P, PACK], BF16, name="w1_grouped", align_bytes=64)
            src = w1_raw[a, b].rearrange("p j (m t) -> p m j t", t=PACK)
            dst = grouped[:].rearrange("p t m j -> p m j t")
            if vector_share > 0:
                nc.vector.tensor_copy(dst[:, 0:vector_share], src[:, 0:vector_share])
            if vector_share < P:
                nc.scalar.copy(dst[:, vector_share:P], src[:, vector_share:P])
            return grouped

        def quantise_w1(a, b, grouped):
            w1_codes[a, b] = held("w1_codes%d%d" % (a, b), [P, K_PASS], U32)
            w1_plane[a, b] = held("w1_plane%d%d" % (a, b), [P, K_PASS], U8)
            nc.vector.quantize_mx(out=w1_codes[a, b][:].bitcast(E4M3X4), scales=w1_plane[a, b][:],
                                  in_=grouped[:].rearrange("p t m j -> p (t m j)"))

        v_codes = [held("v_codes%d" % a, [P, S], U32) for a in range(2)]
        v2_codes = held("v2_codes", [P, S], U32)
        w2_dealt = held("w2_dealt", [P, H], U16)
        a_sum = {}

        def pass_w1(a, b, first, last):
            for s in range(2):
                entries = slice(s * HALF, (s + 1) * HALF)
                for t in range(PACK):
                    cols = slice(t * P, (t + 1) * P)
                    nc.tensor.matmul_mx(out=a_sum[b, s, t // 2][:, t % 2, :],
                                        lhsT=w1_codes[a, b][:, cols].bitcast(E4M3X4),
                                        lhsT_scale=w1_plane[a, b][:, cols],
                                        rhs=v_codes[a][:, entries].bitcast(E4M3X4), rhs_scale=v_plane[a][:, entries],
                                        start=first and t % 2 == 0, stop=last and t % 2 == 1)

        def pass_w2(b, first, last):
            for s in range(2):
                entries = slice(s * HALF, (s + 1) * HALF)
                for t in range(PACK):
                    col0 = b * K_PASS + t * P
                    nc.tensor.matmul_mx(out=a_sum[b, s, t // 2][:, t % 2, :],
                                        lhsT=w2_dealt[:, col0:col0 + P].bitcast(E2M1X4),
                                        lhsT_scale=planes[:, 3 * S + col0:3 * S + col0 + P],
                                        rhs=v2_codes[:, entries].bitcast(E4M3X4), rhs_scale=v2_plane[:, entries],
                                        start=first and t % 2 == 0, stop=last and t % 2 == 1)

        h_codes = [held("h_codes%d" % b, [P, S], U32) for b in range(2)]
        h_plane = [held("h_plane%d" % b, [P, S], U8) for b in range(2)]

        def tanh_half(b, s):
            th = stage.tile([P, PACK, HALF], F32, name="th", bufs=4)
            for t in range(PACK):
                nc.scalar.activation(th[:, t, :], a_sum[b, s, t // 2][:, t % 2, :], TANH,
                                     bias=bias_gain[:, t, b:b + 1])
            return th

        def gain_half(b, th):
            grouped = stage.tile([P, HALF, PACK], BF16, name="h_grouped", align_bytes=64)
            nc.vector.tensor_tensor(
                grouped[:].rearrange("p (c i) t -> p c t i", i=4),
                th[:].rearrange("p t (c i) -> p c t i", i=4),
                bias_gain[:, :, 2 + b].unsqueeze(1).unsqueeze(3).broadcast_to([P, HALF // 4, PACK, 4]),
                MULT)
            return grouped

        def quantise_h(b, s, grouped):
            cols = slice(s * HALF, (s + 1) * HALF)
            nc.vector.quantize_mx(out=h_codes[b][:, cols].bitcast(E4M3X4), scales=h_plane[b][:, cols],
                                  in_=grouped[:].rearrange("p c t -> p (c t)"))

        def round_out_weight(raw, u, pool, name, on_vector):
            grouped = pool.tile([P, 2, P, PACK], BF16, name=name, align_bytes=64)
            c, col0 = divmod(u * P, W_COLS)
            for a in range(2):
                src = raw[a, c][:, :, col0:col0 + P].rearrange("p j (c i) -> p c j i", i=4)
                dst = grouped[:, a].rearrange("p (c i) j -> p c j i", i=4)
                if a >= 2 - on_vector:
                    nc.vector.tensor_copy(dst, src)
                else:
                    nc.scalar.copy(dst, src)
            return grouped

        def quantise_out_weight(grouped, name):
            codes = stage.tile([P, 2 * P], U32, name=name + "_codes", align_bytes=64)
            plane = stage.tile([P, 2 * P], U8, name=name + "_plane", align_bytes=64)
            nc.vector.quantize_mx(out=codes[:].bitcast(E4M3X4), scales=plane[:],
                                  in_=grouped[:].rearrange("p a m j -> p (a m j)"))
            return codes, plane

        def product(weight, moving_codes, moving_plane, col0, width):
            codes, plane = weight
            bank = psum.tile([P, width], F32, name="bank")
            for a in range(2):
                cols = slice(a * P, (a + 1) * P)
                nc.tensor.matmul_mx(out=bank[:], lhsT=codes[:, cols].bitcast(E4M3X4), lhsT_scale=plane[:, cols],
                                    rhs=moving_codes[a][:, col0:col0 + width].bitcast(E4M3X4),
                                    rhs_scale=moving_plane[a][:, col0:col0 + width],
                                    start=(a == 0), stop=(a == 1))
            return bank

        for b in range(2):
            for s in range(2):
                for pair in range(2):
                    a_sum[b, s, pair] = psum.tile([P, 2, HALF], F32, name="bank")

        nc.scalar.copy(w2_dealt[:].rearrange("p (b t m) -> p b t m", b=2, t=PACK),
                       w2_raw[:].rearrange("p (b m t) -> p b t m", b=2, t=PACK))
        quantise_w1(0, 0, round_w1(0, 0, SHARE_00))
        nc.vector.tensor_copy(v_codes[0][:], v_win[0][:].indirect(list1[:]))
        pass_w1(0, 0, True, False)
        nc.vector.tensor_copy(v_codes[1][:], v_win[1][:].indirect(list1[:]))
        quantise_w1(1, 0, round_w1(1, 0, SHARE_10))
        pass_w1(1, 0, False, False)
        for s in range(2):
            nc.vector.tensor_copy(v2_codes[:, s * HALF:(s + 1) * HALF],
                                  v2_win[:].indirect(list2[:, s * HALF // 16:(s + 1) * HALF // 16]))
        pass_w2(0, False, True)
        pass_w2(1, True, False)
        quantise_w1(0, 1, round_w1(0, 1, SHARE_01))
        pass_w1(0, 1, False, False)
        quantise_w1(1, 1, round_w1(1, 1, SHARE_11))
        pass_w1(1, 1, False, True)

        def make_h(b, s):
            quantise_h(b, s, gain_half(b, tanh_half(b, s)))

        def image_product(u):
            w3_q = quantise_out_weight(round_out_weight(w3_raw, u, stage, "w3_grouped", FIRST_W3_ON_VECTOR if u == 0 else 0), "w3")
            return product(w3_q, v_codes, v_plane, 0, S)

        def quantise_w4(u):
            return quantise_out_weight(round_out_weight(w4_raw, u, keep, "swap%d" % (u % 2), FIRST_W4_ON_VECTOR if u == 0 else 0), "w4")

        def put(u, col0, width, p_bank, q_rows, y):
            cols = slice(col0, col0 + width)
            scaled = stage.tile([P, width], F32, name="scaled")
            nc.scalar.activation(scaled[:], p_bank[:], mybir.ActivationFunctionType.Copy, scale=desk_cols[:, u:u + 1])
            nc.vector.tensor_tensor(y[:], q_rows[:, cols], scaled[:], ADD)
            nc.vector.tensor_tensor(pages[u][:].indirect(list3[:, col0 // 16:(col0 + width) // 16]), y[:], wgo_rows[:, cols], MULT)

        make_h(0, 0)
        make_h(0, 1)
        make_h(1, 0)
        q_rows = image_product(0)
        w4_q = quantise_w4(0)
        p_first = product(w4_q, h_codes, h_plane, 0, HALF)
        make_h(1, 1)
        p_bank = product(w4_q, h_codes, h_plane, HALF, HALF)
        put(0, 0, HALF, p_first, q_rows, held("y_first", [P, HALF], F32))
        for u in range(N // P):
            col0 = HALF if u == 0 else 0
            if u + 1 < N // P:
                next_q_rows = image_product(u + 1)
                next_p_bank = product(quantise_w4(u + 1), h_codes, h_plane, 0, S)
            put(u, col0, S - col0, p_bank, q_rows, held("swap%d" % ((u + 1) % 2), [P, S - col0], F32))
            nc.sync.dma_start(out=out[u * P:(u + 1) * P, :], in_=pages[u][:])
            q_rows, p_bank = next_q_rows, next_p_bank
